import numpy as np
import ml_dtypes


def mxq(x, axis, fmt="e4m3"):
    dtype, down = {"e4m3": (ml_dtypes.float8_e4m3fn, 7), "e5m2": (ml_dtypes.float8_e5m2, 14)}[fmt]
    v = np.moveaxis(np.asarray(x, np.float32).astype(ml_dtypes.bfloat16).astype(np.float64), axis, -1)
    blocks = v.reshape(v.shape[:-1] + (-1, 32))
    amax = np.abs(blocks).max(-1, keepdims=True)
    byte = np.maximum(np.where(amax > 0, np.frexp(amax)[1] - 1 + 127, 0) - down, 1)
    scale = np.exp2(byte - 127.0)
    codes = (blocks / scale).astype(np.float32).astype(dtype).astype(np.float64)
    return np.moveaxis((codes * scale).reshape(v.shape), -1, axis)


WIDE = False


def mx_kscale(k):
    if not WIDE:
        return np.ones(k)
    levels = np.array([10, -10, 5, -5, 0])
    if k % 512:
        return np.exp2(np.random.permutation(np.resize(levels, k // 32))).repeat(32)
    a = np.empty((k // 512, 16))
    for p in range(k // 512):
        a[p, :8] = np.random.permutation(np.resize(levels, 8))
        for g in range(8):
            far = levels[np.abs(levels - a[p, g]) >= 10]
            a[p, g + 8] = far[np.random.randint(len(far))]
    return np.exp2(a.ravel()).repeat(32)


def f64(x):
    return np.asarray(x).astype(np.float64)


def striped(idx):
    return np.tile(np.asarray(idx).reshape(-1, 16).T, (8, 1)).astype(np.uint16)


def unstriped(offs):
    return offs[:16].T.reshape(-1).astype(np.int64)


def striped8(idx):
    return np.asarray(idx).reshape(8, -1, 16).transpose(0, 2, 1).reshape(128, -1).astype(np.uint16)


def unstriped8(offs):
    return offs.reshape(8, 16, -1).transpose(0, 2, 1).reshape(8, -1).astype(np.int64)


def pick8(x, idx, run):
    r = np.arange(len(x))
    return x[r[:, None], idx[r % (8 * run) // run]]


E2M1 = np.array([0.0, 0.5, 1.0, 1.5, 2.0, 3.0, 4.0, 6.0, -0.0, -0.5, -1.0, -1.5, -2.0, -3.0, -4.0, -6.0])


def pack_weight(w, fmt):
    k, n = w.shape
    w = f64(np.asarray(w, np.float32).astype(ml_dtypes.bfloat16)).reshape(k // 32, 32, n)
    amax = np.abs(w).max(1)
    if fmt == "e4m3":
        byte = np.frexp(amax)[1] - 1 + 127 - 7
    else:
        mant, ex = np.frexp(amax / 6.0)
        byte = np.where(mant > 0.5, ex, ex - 1) + 127
    byte = np.clip(np.where(amax > 0, byte, 1), 1, 254)
    scaled = (w * np.exp2(127.0 - byte)[:, None, :]).reshape(k, n).astype(np.float32)
    by_word = np.ascontiguousarray(scaled.reshape(k // 512, 128, 4, n).transpose(0, 1, 3, 2))
    if fmt == "e4m3":
        words = by_word.astype(ml_dtypes.float8_e4m3fn).view(np.uint8)
    else:
        c = by_word.astype(ml_dtypes.float4_e2m1fn).view(np.uint8) & 0xF
        words = (c[..., 0::2] | (c[..., 1::2] << 4)).reshape(k // 512, 128, 2 * n)
    return np.ascontiguousarray(words), np.ascontiguousarray(byte.astype(np.uint8).reshape(k // 512, 16, n))


def unpack_weight(words, scales, fmt):
    g, _, n = scales.shape
    words = np.ascontiguousarray(words).reshape(g, 128, n, -1)
    if fmt == "e4m3":
        vals = words.view(ml_dtypes.float8_e4m3fn).astype(np.float64)
    else:
        nib = np.empty((g, 128, n, 4), np.uint8)
        nib[..., 0::2] = words & 0xF
        nib[..., 1::2] = words >> 4
        vals = E2M1[nib]
    vals = vals * np.repeat(np.exp2(scales.astype(np.float64) - 127.0), 8, axis=1)[..., None]
    return vals.transpose(0, 1, 3, 2).reshape(g * 512, n)


K, T, J, S, R, N = 512, 2048, 512, 1024, 512, 512


def setup_inputs():
    n = np.random.standard_normal
    idx = np.random.permutation(T)[:J]
    idx2 = np.stack([np.random.permutation(S)[:J] for _ in range(8)])
    fk = mx_kscale(K)
    fr = mx_kscale(R)
    xtp = pack_weight(n((K, T)) / fk[:, None], "e4m3")
    wap = pack_weight(n((K, R)) * 1 / np.sqrt(K) * fk[:, None] * fr, "e2m1")
    wbp = pack_weight(n((R, N)) * 1 / np.sqrt(R) / fr[:, None], "e4m3")
    return {
        "xt_words": xtp[0],
        "xt_scales": xtp[1],
        "wa_words": wap[0],
        "wa_scales": wap[1],
        "old": (n((R, S)) * 0.7 * fr[:, None]).astype(np.float32),
        "wb_words": wbp[0],
        "wb_scales": wbp[1],
        "offs": striped(idx),
        "offs2": striped8(idx2),
    }


def reference(xt_words, xt_scales, wa_words, wa_scales, old, wb_words, wb_scales, offs, offs2):
    idx = unstriped(offs)
    idx2 = unstriped8(offs2)
    xtu = unpack_weight(xt_words, xt_scales, "e4m3")
    wau = unpack_weight(wa_words, wa_scales, "e2m1")
    wbu = unpack_weight(wb_words, wb_scales, "e4m3")
    xtidxg = xtu[:, idx]
    a = wau.T @ xtidxg
    h1 = np.maximum(a, 0.0)
    hp = np.zeros((R, S))
    hp[np.arange(R)[:, None], idx2[np.arange(R) % 512 // 64]] = h1
    pg = hp + f64(old)
    pgq = mxq(pg, 0, "e4m3")
    y = wbu.T @ pgq
    return y

@@ -1,0 +1,196 @@
+from contextlib import ExitStack
+
+import concourse.mybir as mybir
+
+K, T, J, S, R, N = 512, 2048, 512, 1024, 512, 512
+FLOPS = 2 * K * R * J + 2 * R * N * S
+
+F32 = mybir.dt.float32
+BF16 = mybir.dt.bfloat16
+I32 = mybir.dt.int32
+U32 = mybir.dt.uint32
+U16 = mybir.dt.uint16
+U8 = mybir.dt.uint8
+FP8X4 = mybir.dt.float8_e4m3fn_x4
+FP4X4 = mybir.dt.float4_e2m1fn_x4
+ADD = mybir.AluOpType.add
+RELU = mybir.ActivationFunctionType.Relu
+
+P = 128
+PACK = 4
+BANK = 512
+HALF = J // 2
+CHUNKS = (128, 128, 256, 256, 256)
+BLOCKS_PER_BANK = (2, 4, 2, 2, 2)
+STORE_SPANS = ((0, 0), (1, 1), (2, 2), (3, 4), (3, 4))
+RUN = 128
+
+
+def load_scale_rows(queue, plane, scales, rows=range(4)):
+    for q in rows:
+        queue.dma_start(out=plane[q:P:32, :].bitcast(I32), in_=scales[0][q:16:4, :].bitcast(I32))
+
+
+def tile_moe_expert_hidden_own_places_kernel(
+    tc, xt_words, xt_scales, wa_words, wa_scales, old, wb_words, wb_scales, offs, offs2, out
+):
+    nc = tc.nc
+    with ExitStack() as ctx:
+        lists = ctx.enter_context(tc.tile_pool(name="lists", bufs=1))
+        keep = ctx.enter_context(tc.tile_pool(name="keep", bufs=1))
+        psum = ctx.enter_context(tc.psum_pool(name="psum", bufs=8))
+
+        token_list = lists.tile([P, J // 16], U16, name="token_list")
+        place_lists = lists.tile([P, J // 16], U16, name="place_lists")
+
+        x_words = keep.tile([P, 4 * T], U8, name="x_words", tag="reuse_x_words", align_bytes=64)
+        x_scales = keep.tile([P, T], U8, name="x_scales", align_bytes=64)
+        wa_raw = keep.tile([P, 2 * R], U8, name="wa_raw", tag="reuse_wa", align_bytes=64)
+        wa_scales_raw = keep.tile([P, R], U8, name="wa_scales_raw", align_bytes=64)
+
+        wb = keep.tile([P, 4 * N], U8, name="wb", align_bytes=64)
+        nc.vector.memset(x_scales[:].bitcast(I32), 0)
+        nc.sync.dma_start(out=token_list[:], in_=offs)
+        nc.sync.dma_start(out=wa_raw[:].bitcast(I32), in_=wa_words[0].bitcast(I32))
+        nc.sync.dma_start(out=wb[:].bitcast(I32), in_=wb_words[0].rearrange("p c r -> p (c r)").bitcast(I32))
+        load_scale_rows(nc.sync, x_scales, xt_scales)
+        nc.sync.dma_start(out=x_words[:].bitcast(I32), in_=xt_words[0].rearrange("p c r -> p (c r)").bitcast(I32))
+        pages = [keep.tile([P, S], F32, name=f"page{t}") for t in range(PACK)]
+        nc.vector.memset(pages[0][:], 0.0)
+        nc.vector.memset(wa_scales_raw[:].bitcast(I32), 0)
+        load_scale_rows(nc.scalar, wa_scales_raw, wa_scales)
+        nc.sync.dma_start(out=place_lists[:], in_=offs2)
+        for t in range(1, PACK):
+            nc.vector.memset(pages[t][:], 0.0)
+        wb_plane = keep.tile([P, N], U8, name="wb_plane", align_bytes=64)
+        nc.vector.memset(wb_plane[:].bitcast(I32), 0)
+
+        wa_turned = keep.tile([P, 2 * R], U8, name="wa_turned", align_bytes=64)
+        wa_scales_turned = keep.tile([P, R], U8, name="wa_scales_turned", align_bytes=64)
+        nc.vector.tensor_copy(
+            out=wa_turned[:].bitcast(U16).rearrange("p (t m) -> p t m", t=PACK),
+            in_=wa_raw[:].bitcast(U16).rearrange("p (m t) -> p t m", t=PACK),
+        )
+        slot_words = keep.tile([P, J], U32, name="slot_words", align_bytes=64)
+        slot_scales = keep.tile([P, J], U8, name="slot_scales", align_bytes=64)
+        nc.vector.tensor_copy(out=slot_scales[:], in_=x_scales[:].indirect(token_list[:]))
+        nc.vector.tensor_copy(
+            out=wa_scales_turned[:].rearrange("p (t m) -> p t m", t=PACK),
+            in_=wa_scales_raw[:].rearrange("p (m t) -> p t m", t=PACK),
+        )
+        for h in range(2):
+            nc.vector.tensor_copy(
+                out=slot_words[:, h * HALF : (h + 1) * HALF],
+                in_=x_words[:].bitcast(U32).indirect(token_list[:, h * HALF // 16 : (h + 1) * HALF // 16]),
+            )
+
+        old_rows = old.rearrange("(p t) s -> p t s", t=PACK)
+        old_low = keep.tile([P, 2, S], F32, name="old_low", tag="reuse_wa", align_bytes=64)
+        nc.sync.dma_start(out=old_low[:], in_=old_rows[:, 0:2, :])
+        load_scale_rows(nc.sync, wb_plane, wb_scales)
+        old_high = keep.tile([P, 2, S], F32, name="old_high", tag="reuse_x_words", align_bytes=64)
+        nc.sync.dma_start(out=old_high[:], in_=old_rows[:, 2:4, :])
+
+        hidden = [keep.tile([P, J], F32, name=f"hidden{t}", align_bytes=64) for t in range(PACK)]
+        pieces = [(0, 0, HALF), (0, HALF, J)] + [(t, 0, J) for t in range(1, PACK)]
+        for t, j0, j1 in pieces:
+            acc = psum.tile([P, BANK], F32, name="acc")
+            nc.tensor.matmul_mx(
+                out=acc[:, 0 : j1 - j0],
+                lhsT=wa_turned[:, 2 * P * t : 2 * P * (t + 1)].bitcast(FP4X4),
+                lhsT_scale=wa_scales_turned[:, P * t : P * (t + 1)],
+                rhs=slot_words[:, j0:j1].bitcast(FP8X4),
+                rhs_scale=slot_scales[:, j0:j1],
+                start=True,
+                stop=True,
+            )
+            nc.scalar.activation(out=hidden[t][:, j0:j1], in_=acc[:, 0 : j1 - j0], func=RELU)
+        for t, j0, j1 in pieces:
+            nc.vector.tensor_copy(
+                out=pages[t][:].indirect(place_lists[:, j0 // 16 : j1 // 16]), in_=hidden[t][:, j0:j1]
+            )
+
+        starts = [sum(CHUNKS[:c]) for c in range(len(CHUNKS))]
+        cols = [slice(s0, s0 + w) for s0, w in zip(starts, CHUNKS)]
+        sums_low = keep.tile([P, 2, S], BF16, name="sums_low")
+        for t in range(2):
+            nc.gpsimd.tensor_tensor(out=sums_low[:, t, :], in0=pages[t][:], in1=old_low[:, t, :], op=ADD)
+        grouped = [keep.tile([P, w, PACK], BF16, name=f"grouped{c}", align_bytes=64) for c, w in enumerate(CHUNKS)]
+        for c in range(len(CHUNKS)):
+            nc.scalar.copy(out=grouped[c][:, :, 0:2], in_=sums_low[:, :, cols[c]].rearrange("p t s -> p s t"))
+        sums_high = keep.tile([P, 2 * S], BF16, name="sums_high")
+        high_runs = sums_high[:].rearrange("p (u t s) -> p u t s", t=2, s=RUN)
+        nc.gpsimd.tensor_tensor(
+            out=high_runs[:, :, 0, :],
+            in0=pages[2][:].rearrange("p (u s) -> p u s", s=RUN),
+            in1=old_high[:, 0, :].rearrange("p (u s) -> p u s", s=RUN),
+            op=ADD,
+        )
+
+        codes = [keep.tile([P, w], U32, name=f"codes{c}", align_bytes=64) for c, w in enumerate(CHUNKS)]
+        planes = [keep.tile([P, w], U8, name=f"plane{c}", align_bytes=64) for c, w in enumerate(CHUNKS)]
+        out_rows = out.rearrange("(b p) s -> p b s", p=P)
+
+        def runs(c):
+            return slice(starts[c] // RUN, (starts[c] + CHUNKS[c]) // RUN)
+
+        def add_last(c):
+            nc.vector.tensor_tensor(
+                out=high_runs[:, runs(c), 1, :],
+                in0=pages[3][:, cols[c]].rearrange("p (u s) -> p u s", s=RUN),
+                in1=old_high[:, 1, cols[c]].rearrange("p (u s) -> p u s", s=RUN),
+                op=ADD,
+            )
+
+        def weave(c):
+            nc.vector.tensor_copy(
+                out=grouped[c][:, :, 2:4].rearrange("p (u s) t -> p u s t", s=RUN),
+                in_=high_runs[:, runs(c), :, :].rearrange("p u t s -> p u s t"),
+            )
+
+        def quantise(c):
+            nc.vector.quantize_mx(
+                out=codes[c][:].bitcast(FP8X4), scales=planes[c][:], in_=grouped[c][:].rearrange("p s t -> p (s t)")
+            )
+
+        results = {}
+
+        def second_layer(c):
+            w = CHUNKS[c]
+            per_bank = BLOCKS_PER_BANK[c]
+            first, last = STORE_SPANS[c]
+            s0, s1 = starts[first], starts[last] + CHUNKS[last]
+            for b0 in range(0, N // P, per_bank):
+                acc = psum.tile([P, BANK], F32, name="acc")
+                for i in range(per_bank):
+                    b = b0 + i
+                    nc.tensor.matmul_mx(
+                        out=acc[:, i * w : (i + 1) * w],
+                        lhsT=wb[:, 4 * P * b : 4 * P * (b + 1)].bitcast(FP8X4),
+                        lhsT_scale=wb_plane[:, P * b : P * (b + 1)],
+                        rhs=codes[c][:].bitcast(FP8X4),
+                        rhs_scale=planes[c][:],
+                        start=True,
+                        stop=True,
+                    )
+                if c == first:
+                    results[b0] = keep.tile([P, per_bank, s1 - s0], F32, name=f"result{c}_{b0}")
+                target = results[b0][:, :, starts[c] - s0 : starts[c] - s0 + w]
+                sums = acc[:, 0 : per_bank * w].rearrange("p (b s) -> p b s", s=w)
+                if c == len(CHUNKS) - 1 and b0 == 0:
+                    nc.vector.tensor_copy(out=target, in_=sums)
+                else:
+                    nc.scalar.copy(out=target, in_=sums)
+                if c == last:
+                    nc.sync.dma_start(out=out_rows[:, b0 : b0 + per_bank, s0:s1], in_=results[b0][:])
+
+        add_last(0)
+        add_last(1)
+        weave(0)
+        for c in range(len(CHUNKS)):
+            if c + 1 < len(CHUNKS):
+                weave(c + 1)
+            quantise(c)
+            if c + 2 < len(CHUNKS):
+                add_last(c + 2)
+            second_layer(c)

@@ -41,70 +41,76 @@ def tile_moe_expert_hidden_own_places_kernel(
         psum = ctx.enter_context(tc.psum_pool(name="psum", bufs=8))
 
         token_list = lists.tile([P, J // 16], U16, name="token_list")
-        place_lists = lists.tile([P, J // 16], U16, name="place_lists")
 
         x_words = keep.tile([P, 4 * T], U8, name="x_words", tag="reuse_x_words", align_bytes=64)
-        x_scales = keep.tile([P, T], U8, name="x_scales", align_bytes=64)
-        wa_raw = keep.tile([P, 2 * R], U8, name="wa_raw", tag="reuse_wa", align_bytes=64)
-        wa_scales_raw = keep.tile([P, R], U8, name="wa_scales_raw", align_bytes=64)
+        x_scales = keep.tile([P, T], U8, name="x_scales", tag="reuse_x_scales", align_bytes=64)
+        wa_raw = keep.tile([P, 2 * R], U8, name="wa_raw", align_bytes=64)
+        wa_scales_raw = keep.tile([P, R], U8, name="wa_scales_raw", tag="reuse_wa_scales", align_bytes=64)
 
         wb = keep.tile([P, 4 * N], U8, name="wb", align_bytes=64)
         nc.vector.memset(x_scales[:].bitcast(I32), 0)
         nc.sync.dma_start(out=token_list[:], in_=offs)
         nc.sync.dma_start(out=wa_raw[:].bitcast(I32), in_=wa_words[0].bitcast(I32))
         nc.sync.dma_start(out=wb[:].bitcast(I32), in_=wb_words[0].rearrange("p c r -> p (c r)").bitcast(I32))
-        load_scale_rows(nc.sync, x_scales, xt_scales)
+        load_scale_rows(nc.sync, x_scales, xt_scales, (0, 1))
+        load_scale_rows(nc.scalar, x_scales, xt_scales, (2, 3))
         nc.sync.dma_start(out=x_words[:].bitcast(I32), in_=xt_words[0].rearrange("p c r -> p (c r)").bitcast(I32))
-        pages = [keep.tile([P, S], F32, name=f"page{t}") for t in range(PACK)]
-        nc.vector.memset(pages[0][:], 0.0)
+        pages = [keep.tile([P, S], F32, name=f"page{t}") for t in range(2)]
+        for t in range(2):
+            nc.vector.memset(pages[t][:], 0.0)
         nc.vector.memset(wa_scales_raw[:].bitcast(I32), 0)
         load_scale_rows(nc.scalar, wa_scales_raw, wa_scales)
+        place_lists = lists.tile([P, J // 16], U16, name="place_lists")
         nc.sync.dma_start(out=place_lists[:], in_=offs2)
-        for t in range(1, PACK):
-            nc.vector.memset(pages[t][:], 0.0)
         wb_plane = keep.tile([P, N], U8, name="wb_plane", align_bytes=64)
         nc.vector.memset(wb_plane[:].bitcast(I32), 0)
 
-        wa_turned = keep.tile([P, 2 * R], U8, name="wa_turned", align_bytes=64)
-        wa_scales_turned = keep.tile([P, R], U8, name="wa_scales_turned", align_bytes=64)
+        wa_turned = keep.tile([P, 2 * R], U8, name="wa_turned", tag="reuse_wa_turned", align_bytes=64)
+        wa_scales_turned = keep.tile([P, R], U8, name="wa_scales_turned", tag="reuse_wa_scales_turned", align_bytes=64)
         nc.vector.tensor_copy(
             out=wa_turned[:].bitcast(U16).rearrange("p (t m) -> p t m", t=PACK),
             in_=wa_raw[:].bitcast(U16).rearrange("p (m t) -> p t m", t=PACK),
         )
-        slot_words = keep.tile([P, J], U32, name="slot_words", align_bytes=64)
         slot_scales = keep.tile([P, J], U8, name="slot_scales", align_bytes=64)
         nc.vector.tensor_copy(out=slot_scales[:], in_=x_scales[:].indirect(token_list[:]))
         nc.vector.tensor_copy(
             out=wa_scales_turned[:].rearrange("p (t m) -> p t m", t=PACK),
             in_=wa_scales_raw[:].rearrange("p (m t) -> p t m", t=PACK),
         )
-        for h in range(2):
+        slot_words = []
+        for h, tag in enumerate(("slot_words", "reuse_wa_scales")):
+            slot_words.append(keep.tile([P, HALF], U32, name=f"slot_words{h}", tag=tag, align_bytes=64))
             nc.vector.tensor_copy(
-                out=slot_words[:, h * HALF : (h + 1) * HALF],
+                out=slot_words[h][:],
                 in_=x_words[:].bitcast(U32).indirect(token_list[:, h * HALF // 16 : (h + 1) * HALF // 16]),
             )
 
         old_rows = old.rearrange("(p t) s -> p t s", t=PACK)
-        old_low = keep.tile([P, 2, S], F32, name="old_low", tag="reuse_wa", align_bytes=64)
+        old_low = keep.tile([P, 2, S], F32, name="old_low", tag="reuse_x_scales", align_bytes=64)
         nc.sync.dma_start(out=old_low[:], in_=old_rows[:, 0:2, :])
         load_scale_rows(nc.sync, wb_plane, wb_scales)
         old_high = keep.tile([P, 2, S], F32, name="old_high", tag="reuse_x_words", align_bytes=64)
         nc.sync.dma_start(out=old_high[:], in_=old_rows[:, 2:4, :])
 
         hidden = [keep.tile([P, J], F32, name=f"hidden{t}", align_bytes=64) for t in range(PACK)]
-        pieces = [(0, 0, HALF), (0, HALF, J)] + [(t, 0, J) for t in range(1, PACK)]
+        pieces = [(0, 0, P), (0, P, HALF), (0, HALF, J)] + [(t, 0, J) for t in range(1, PACK)]
         for t, j0, j1 in pieces:
             acc = psum.tile([P, BANK], F32, name="acc")
-            nc.tensor.matmul_mx(
-                out=acc[:, 0 : j1 - j0],
-                lhsT=wa_turned[:, 2 * P * t : 2 * P * (t + 1)].bitcast(FP4X4),
-                lhsT_scale=wa_scales_turned[:, P * t : P * (t + 1)],
-                rhs=slot_words[:, j0:j1].bitcast(FP8X4),
-                rhs_scale=slot_scales[:, j0:j1],
-                start=True,
-                stop=True,
-            )
+            for a0 in range(j0, j1, HALF):
+                a1 = min(j1, a0 + HALF)
+                nc.tensor.matmul_mx(
+                    out=acc[:, a0 - j0 : a1 - j0],
+                    lhsT=wa_turned[:, 2 * P * t : 2 * P * (t + 1)].bitcast(FP4X4),
+                    lhsT_scale=wa_scales_turned[:, P * t : P * (t + 1)],
+                    rhs=slot_words[a0 // HALF][:, a0 % HALF : a0 % HALF + a1 - a0].bitcast(FP8X4),
+                    rhs_scale=slot_scales[:, a0:a1],
+                    start=True,
+                    stop=True,
+                )
             nc.scalar.activation(out=hidden[t][:, j0:j1], in_=acc[:, 0 : j1 - j0], func=RELU)
+        for t, tag in ((2, "reuse_wa_turned"), (3, "reuse_wa_scales_turned")):
+            pages.append(keep.tile([P, S], F32, name=f"page{t}", tag=tag, align_bytes=64))
+            nc.gpsimd.memset(pages[t][:], 0.0)
         for t, j0, j1 in pieces:
             nc.vector.tensor_copy(
                 out=pages[t][:].indirect(place_lists[:, j0 // 16 : j1 // 16]), in_=hidden[t][:, j0:j1]

from contextlib import ExitStack

import concourse.mybir as mybir

K, T, J, S, R, N = 512, 2048, 512, 1024, 512, 512
FLOPS = 2 * K * R * J + 2 * R * N * S

F32 = mybir.dt.float32
BF16 = mybir.dt.bfloat16
I32 = mybir.dt.int32
U32 = mybir.dt.uint32
U16 = mybir.dt.uint16
U8 = mybir.dt.uint8
FP8X4 = mybir.dt.float8_e4m3fn_x4
FP4X4 = mybir.dt.float4_e2m1fn_x4
ADD = mybir.AluOpType.add
RELU = mybir.ActivationFunctionType.Relu

P = 128
PACK = 4
BANK = 512
HALF = J // 2
CHUNKS = (128, 128, 256, 256, 256)
BLOCKS_PER_BANK = (2, 4, 2, 2, 2)
STORE_SPANS = ((0, 0), (1, 1), (2, 2), (3, 4), (3, 4))
RUN = 128


def load_scale_rows(queue, plane, scales, rows=range(4)):
    for q in rows:
        queue.dma_start(out=plane[q:P:32, :].bitcast(I32), in_=scales[0][q:16:4, :].bitcast(I32))


def tile_moe_expert_hidden_own_places_kernel(
    tc, xt_words, xt_scales, wa_words, wa_scales, old, wb_words, wb_scales, offs, offs2, out
):
    nc = tc.nc
    with ExitStack() as ctx:
        lists = ctx.enter_context(tc.tile_pool(name="lists", bufs=1))
        keep = ctx.enter_context(tc.tile_pool(name="keep", bufs=1))
        psum = ctx.enter_context(tc.psum_pool(name="psum", bufs=8))

        token_list = lists.tile([P, J // 16], U16, name="token_list")

        x_words = keep.tile([P, 4 * T], U8, name="x_words", tag="reuse_x_words", align_bytes=64)
        x_scales = keep.tile([P, T], U8, name="x_scales", tag="reuse_x_scales", align_bytes=64)
        wa_raw = keep.tile([P, 2 * R], U8, name="wa_raw", align_bytes=64)
        wa_scales_raw = keep.tile([P, R], U8, name="wa_scales_raw", tag="reuse_wa_scales", align_bytes=64)

        wb = keep.tile([P, 4 * N], U8, name="wb", align_bytes=64)
        nc.vector.memset(x_scales[:].bitcast(I32), 0)
        nc.sync.dma_start(out=token_list[:], in_=offs)
        nc.sync.dma_start(out=wa_raw[:].bitcast(I32), in_=wa_words[0].bitcast(I32))
        nc.sync.dma_start(out=wb[:].bitcast(I32), in_=wb_words[0].rearrange("p c r -> p (c r)").bitcast(I32))
        load_scale_rows(nc.sync, x_scales, xt_scales, (0, 1))
        load_scale_rows(nc.scalar, x_scales, xt_scales, (2, 3))
        nc.sync.dma_start(out=x_words[:].bitcast(I32), in_=xt_words[0].rearrange("p c r -> p (c r)").bitcast(I32))
        pages = [keep.tile([P, S], F32, name=f"page{t}") for t in range(2)]
        for t in range(2):
            nc.vector.memset(pages[t][:], 0.0)
        nc.vector.memset(wa_scales_raw[:].bitcast(I32), 0)
        load_scale_rows(nc.scalar, wa_scales_raw, wa_scales)
        place_lists = lists.tile([P, J // 16], U16, name="place_lists")
        nc.sync.dma_start(out=place_lists[:], in_=offs2)
        wb_plane = keep.tile([P, N], U8, name="wb_plane", align_bytes=64)
        nc.vector.memset(wb_plane[:].bitcast(I32), 0)

        wa_turned = keep.tile([P, 2 * R], U8, name="wa_turned", tag="reuse_wa_turned", align_bytes=64)
        wa_scales_turned = keep.tile([P, R], U8, name="wa_scales_turned", tag="reuse_wa_scales_turned", align_bytes=64)
        nc.vector.tensor_copy(
            out=wa_turned[:].bitcast(U16).rearrange("p (t m) -> p t m", t=PACK),
            in_=wa_raw[:].bitcast(U16).rearrange("p (m t) -> p t m", t=PACK),
        )
        slot_scales = keep.tile([P, J], U8, name="slot_scales", align_bytes=64)
        nc.vector.tensor_copy(out=slot_scales[:], in_=x_scales[:].indirect(token_list[:]))
        nc.vector.tensor_copy(
            out=wa_scales_turned[:].rearrange("p (t m) -> p t m", t=PACK),
            in_=wa_scales_raw[:].rearrange("p (m t) -> p t m", t=PACK),
        )
        slot_words = []
        for h, tag in enumerate(("slot_words", "reuse_wa_scales")):
            slot_words.append(keep.tile([P, HALF], U32, name=f"slot_words{h}", tag=tag, align_bytes=64))
            nc.vector.tensor_copy(
                out=slot_words[h][:],
                in_=x_words[:].bitcast(U32).indirect(token_list[:, h * HALF // 16 : (h + 1) * HALF // 16]),
            )

        old_rows = old.rearrange("(p t) s -> p t s", t=PACK)
        old_low = keep.tile([P, 2, S], F32, name="old_low", tag="reuse_x_scales", align_bytes=64)
        nc.sync.dma_start(out=old_low[:], in_=old_rows[:, 0:2, :])
        load_scale_rows(nc.sync, wb_plane, wb_scales)
        old_high = keep.tile([P, 2, S], F32, name="old_high", tag="reuse_x_words", align_bytes=64)
        nc.sync.dma_start(out=old_high[:], in_=old_rows[:, 2:4, :])

        hidden = [keep.tile([P, J], F32, name=f"hidden{t}", align_bytes=64) for t in range(PACK)]
        pieces = [(0, 0, P), (0, P, HALF), (0, HALF, J)] + [(t, 0, J) for t in range(1, PACK)]
        for t, j0, j1 in pieces:
            acc = psum.tile([P, BANK], F32, name="acc")
            for a0 in range(j0, j1, HALF):
                a1 = min(j1, a0 + HALF)
                nc.tensor.matmul_mx(
                    out=acc[:, a0 - j0 : a1 - j0],
                    lhsT=wa_turned[:, 2 * P * t : 2 * P * (t + 1)].bitcast(FP4X4),
                    lhsT_scale=wa_scales_turned[:, P * t : P * (t + 1)],
                    rhs=slot_words[a0 // HALF][:, a0 % HALF : a0 % HALF + a1 - a0].bitcast(FP8X4),
                    rhs_scale=slot_scales[:, a0:a1],
                    start=True,
                    stop=True,
                )
            nc.scalar.activation(out=hidden[t][:, j0:j1], in_=acc[:, 0 : j1 - j0], func=RELU)
        for t, tag in ((2, "reuse_wa_turned"), (3, "reuse_wa_scales_turned")):
            pages.append(keep.tile([P, S], F32, name=f"page{t}", tag=tag, align_bytes=64))
            nc.gpsimd.memset(pages[t][:], 0.0)
        for t, j0, j1 in pieces:
            nc.vector.tensor_copy(
                out=pages[t][:].indirect(place_lists[:, j0 // 16 : j1 // 16]), in_=hidden[t][:, j0:j1]
            )

        starts = [sum(CHUNKS[:c]) for c in range(len(CHUNKS))]
        cols = [slice(s0, s0 + w) for s0, w in zip(starts, CHUNKS)]
        sums_low = keep.tile([P, 2, S], BF16, name="sums_low")
        for t in range(2):
            nc.gpsimd.tensor_tensor(out=sums_low[:, t, :], in0=pages[t][:], in1=old_low[:, t, :], op=ADD)
        grouped = [keep.tile([P, w, PACK], BF16, name=f"grouped{c}", align_bytes=64) for c, w in enumerate(CHUNKS)]
        for c in range(len(CHUNKS)):
            nc.scalar.copy(out=grouped[c][:, :, 0:2], in_=sums_low[:, :, cols[c]].rearrange("p t s -> p s t"))
        sums_high = keep.tile([P, 2 * S], BF16, name="sums_high")
        high_runs = sums_high[:].rearrange("p (u t s) -> p u t s", t=2, s=RUN)
        nc.gpsimd.tensor_tensor(
            out=high_runs[:, :, 0, :],
            in0=pages[2][:].rearrange("p (u s) -> p u s", s=RUN),
            in1=old_high[:, 0, :].rearrange("p (u s) -> p u s", s=RUN),
            op=ADD,
        )

        codes = [keep.tile([P, w], U32, name=f"codes{c}", align_bytes=64) for c, w in enumerate(CHUNKS)]
        planes = [keep.tile([P, w], U8, name=f"plane{c}", align_bytes=64) for c, w in enumerate(CHUNKS)]
        out_rows = out.rearrange("(b p) s -> p b s", p=P)

        def runs(c):
            return slice(starts[c] // RUN, (starts[c] + CHUNKS[c]) // RUN)

        def add_last(c):
            nc.vector.tensor_tensor(
                out=high_runs[:, runs(c), 1, :],
                in0=pages[3][:, cols[c]].rearrange("p (u s) -> p u s", s=RUN),
                in1=old_high[:, 1, cols[c]].rearrange("p (u s) -> p u s", s=RUN),
                op=ADD,
            )

        def weave(c):
            nc.vector.tensor_copy(
                out=grouped[c][:, :, 2:4].rearrange("p (u s) t -> p u s t", s=RUN),
                in_=high_runs[:, runs(c), :, :].rearrange("p u t s -> p u s t"),
            )

        def quantise(c):
            nc.vector.quantize_mx(
                out=codes[c][:].bitcast(FP8X4), scales=planes[c][:], in_=grouped[c][:].rearrange("p s t -> p (s t)")
            )

        results = {}

        def second_layer(c):
            w = CHUNKS[c]
            per_bank = BLOCKS_PER_BANK[c]
            first, last = STORE_SPANS[c]
            s0, s1 = starts[first], starts[last] + CHUNKS[last]
            for b0 in range(0, N // P, per_bank):
                acc = psum.tile([P, BANK], F32, name="acc")
                for i in range(per_bank):
                    b = b0 + i
                    nc.tensor.matmul_mx(
                        out=acc[:, i * w : (i + 1) * w],
                        lhsT=wb[:, 4 * P * b : 4 * P * (b + 1)].bitcast(FP8X4),
                        lhsT_scale=wb_plane[:, P * b : P * (b + 1)],
                        rhs=codes[c][:].bitcast(FP8X4),
                        rhs_scale=planes[c][:],
                        start=True,
                        stop=True,
                    )
                if c == first:
                    results[b0] = keep.tile([P, per_bank, s1 - s0], F32, name=f"result{c}_{b0}")
                target = results[b0][:, :, starts[c] - s0 : starts[c] - s0 + w]
                sums = acc[:, 0 : per_bank * w].rearrange("p (b s) -> p b s", s=w)
                if c == len(CHUNKS) - 1 and b0 == 0:
                    nc.vector.tensor_copy(out=target, in_=sums)
                else:
                    nc.scalar.copy(out=target, in_=sums)
                if c == last:
                    nc.sync.dma_start(out=out_rows[:, b0 : b0 + per_bank, s0:s1], in_=results[b0][:])

        add_last(0)
        add_last(1)
        weave(0)
        for c in range(len(CHUNKS)):
            if c + 1 < len(CHUNKS):
                weave(c + 1)
            quantise(c)
            if c + 2 < len(CHUNKS):
                add_last(c + 2)
            second_layer(c)
